import numpy as np
import ml_dtypes


def mxq(x, axis, fmt="e4m3"):
    dtype, down = {"e4m3": (ml_dtypes.float8_e4m3fn, 7), "e5m2": (ml_dtypes.float8_e5m2, 14)}[fmt]
    v = np.moveaxis(np.asarray(x, np.float32).astype(ml_dtypes.bfloat16).astype(np.float64), axis, -1)
    blocks = v.reshape(v.shape[:-1] + (-1, 32))
    amax = np.abs(blocks).max(-1, keepdims=True)
    byte = np.maximum(np.where(amax > 0, np.frexp(amax)[1] - 1 + 127, 0) - down, 1)
    scale = np.exp2(byte - 127.0)
    codes = (blocks / scale).astype(np.float32).astype(dtype).astype(np.float64)
    return np.moveaxis((codes * scale).reshape(v.shape), -1, axis)


WIDE = False


def mx_kscale(k):
    if not WIDE:
        return np.ones(k)
    levels = np.array([10, -10, 5, -5, 0])
    if k % 512:
        return np.exp2(np.random.permutation(np.resize(levels, k // 32))).repeat(32)
    a = np.empty((k // 512, 16))
    for p in range(k // 512):
        a[p, :8] = np.random.permutation(np.resize(levels, 8))
        for g in range(8):
            far = levels[np.abs(levels - a[p, g]) >= 10]
            a[p, g + 8] = far[np.random.randint(len(far))]
    return np.exp2(a.ravel()).repeat(32)


def f64(x):
    return np.asarray(x).astype(np.float64)


def striped(idx):
    return np.tile(idx.reshape(-1, 16).T, (8, 1)).astype(np.uint16)


def unstriped(offs):
    return offs[:16].T.reshape(-1).astype(np.int64)


def gelu(v):
    return 0.5 * v * (1.0 + np.tanh(np.sqrt(2.0 / np.pi) * (v + 0.044715 * v**3)))


K, T, E, C, H, N = 2048, 512, 2, 256, 512, 512


def by_expert(wq, xq):
    return np.concatenate([wq[e].T @ xq[:, e * C:(e + 1) * C] for e in range(E)], axis=1)


def setup_inputs():
    n = np.random.standard_normal
    s = mx_kscale(K)[:, None]
    u = mx_kscale(H)
    return {
        "xT": (n((K, T)) * s).astype(np.float32),
        "w1": (n((E, K, H)) / np.sqrt(K) / s[None]).astype(np.float32),
        "w3": (n((E, K, H)) / np.sqrt(K) / s[None] * u[None, None, :]).astype(np.float32),
        "w2": (n((E, H, N)) / np.sqrt(H) / u[None, :, None]).astype(np.float32),
        "gate": np.tile(np.random.uniform(0.2, 1.0, E * C), (N, 1)).astype(np.float32),
        "offs": striped(np.random.permutation(T)[:E * C]),
    }


def reference(xT, w1, w3, w2, gate, offs):
    idx = unstriped(offs)
    xq = mxq(f64(xT)[:, idx], 0, "e4m3")
    h = gelu(by_expert(mxq(f64(w1), 1, "e4m3"), xq))
    h = h * by_expert(mxq(f64(w3), 1, "e4m3"), xq)
    y = by_expert(mxq(f64(w2), 1, "e4m3"), mxq(h, 0, "e4m3"))
    out = np.zeros((N, T))
    out[:, idx] = f64(gate) * y
    return out

@@ -1,0 +1,241 @@
+from contextlib import ExitStack
+
+import concourse.mybir as mybir
+
+K, T, E, C, H, N = 2048, 512, 2, 256, 512, 512
+FLOPS = 2 * E * C * (2 * K * H + H * N)
+
+F32 = mybir.dt.float32
+BF16 = mybir.dt.bfloat16
+U32 = mybir.dt.uint32
+U16 = mybir.dt.uint16
+U8 = mybir.dt.uint8
+FP8X4 = mybir.dt.float8_e4m3fn_x4
+MULT = mybir.AluOpType.mult
+GELU = mybir.ActivationFunctionType.Gelu_apprx_tanh
+
+P = 128
+PACK = 4
+KP = P * PACK
+PASSES = K // KP
+LISTC = C // 16
+VECTOR_SHARE = {("w1", 0): (0, 16, 0, 16), ("w3", 0): (0, 16, 0, 16), ("w1", 1): (0, 16, 0, 16), ("w3", 1): (0, 16, 8, 16)}
+
+
+def tile_routed_moe_kernel(tc, xT, w1, w3, w2, gate, offs, out):
+    nc = tc.nc
+    with ExitStack() as ctx:
+        keep = ctx.enter_context(tc.tile_pool(name="keep", bufs=1))
+        raw_pool = ctx.enter_context(tc.tile_pool(name="raw", bufs=8))
+        il_pool = ctx.enter_context(tc.tile_pool(name="il", bufs=4))
+        act_pool = ctx.enter_context(tc.tile_pool(name="act", bufs=2))
+        y_pool = ctx.enter_context(tc.tile_pool(name="y", bufs=4))
+        psum = ctx.enter_context(tc.psum_pool(name="psum", bufs=1))
+
+        offsets = keep.tile([P, E * LISTC], U16, name="offsets")
+        nc.sync.dma_start(offsets[:], offs)
+        warm = keep.tile([P, 1], F32, name="warm")
+        nc.gpsimd.memset(warm[:], 0.0)
+        nc.scalar.activation(warm[:], warm[:], GELU)
+        x_scales = keep.tile([P, T], U8, name="x_scales", align_bytes=64)
+        nc.gpsimd.memset(x_scales[:], 0)
+
+        def natural(eng, il, raw, c0, c1):
+            o = il[:].rearrange("p (c i j) -> p c j i", i=4, j=4)[:, c0 // 4 : c1 // 4]
+            i = raw[:].rearrange("p j (c i) -> p c j i", i=4)[:, c0 // 4 : c1 // 4]
+            eng(o, i)
+
+        def permuted(eng, il, raw, q0, q1):
+            o = il[:].rearrange("p (t q s j) -> p t q j s", t=4, s=4, j=4)[:, :, q0:q1]
+            i = raw[:].rearrange("p j (q t s) -> p t q j s", t=4, s=4)[:, :, q0:q1]
+            eng(o, i)
+
+
+        steps = [("x", 0, s) for s in range(PASSES)]
+        for e in range(E):
+            steps += [("w1", e, s) for s in range(PASSES)]
+            steps += [("w3", e, s) for s in range(PASSES)]
+            steps += [("w2", e, 0)]
+        n_steps = len(steps)
+        dram = {"w1": w1, "w3": w3}
+
+        raws, ils, codes = {}, {}, {}
+        gates = {}
+
+        def load(i):
+            kind, e, s = steps[i]
+            raw = raw_pool.tile([P, PACK, 512], F32, name="raw", tag="raw")
+            raws[i] = raw
+            if kind == "w2":
+                rows = w2[e].rearrange("(q t s) n -> s q t n", t=4, s=4)
+                for s in range(4):
+                    nc.sync.dma_start(raw[s::4], rows[s])
+                gt = keep.tile([P, 4, C], F32, name=f"gate{e}")
+                nc.sync.dma_start(gt[:], gate[:, e * C : (e + 1) * C].rearrange("(n p) c -> p n c", p=P))
+                gates[e] = gt
+                return
+            if kind == "x":
+                src = xT[s * KP : (s + 1) * KP, :].rearrange("(p j) t -> p j t", j=PACK)
+            else:
+                src = dram[kind][e, s * KP : (s + 1) * KP, :].rearrange("(p j) c -> p j c", j=PACK)
+            if i == n_steps - 2:
+                nc.sync.dma_start(raw[:, :, 256:], src[:, :, 256:])
+                nc.sync.dma_start(raw[:, :, :256], src[:, :, :256])
+            else:
+                nc.sync.dma_start(raw[:], src)
+
+        def round_(i):
+            kind, e, s = steps[i]
+            raw = raws[i]
+            il = il_pool.tile([P, PACK * 512], BF16, name="il", tag="il", align_bytes=64)
+            ils[i] = il
+            if kind == "x":
+                natural(nc.vector.tensor_copy, il, raw, 0, 192)
+                natural(nc.scalar.copy, il, raw, 192, 512)
+            elif kind == "w2":
+                if e == 0:
+                    natural(nc.vector.tensor_copy, il, raw, 0, 512)
+                else:
+                    natural(nc.scalar.copy, il, raw, 0, 256)
+                    natural(nc.scalar.copy, il, raw, 256, 512)
+            else:
+                split = VECTOR_SHARE[kind, e][s]
+                if split:
+                    permuted(nc.vector.tensor_copy, il, raw, 0, split)
+                permuted(nc.scalar.copy, il, raw, split, 32)
+
+        def quantize(i):
+            kind, e, s = steps[i]
+            il = ils[i]
+            words = keep.tile([P, 512], U32, name=f"words_{kind}_{e}_{s}", align_bytes=64)
+            if kind == "x":
+                scales = x_scales
+                nc.vector.quantize_mx(words[:].bitcast(FP8X4), x_scales[4 * s : P, :], il[:])
+            else:
+                scales = keep.tile([P, 512], U8, name=f"scales_{kind}_{e}_{s}", align_bytes=64)
+                cuts = (0, 256, 512) if kind == "w2" and e == 1 else (0, 512)
+                for c0, c1 in zip(cuts[:-1], cuts[1:]):
+                    nc.vector.quantize_mx(words[:, c0:c1].bitcast(FP8X4), scales[:, c0:c1], il[:, 4 * c0 : 4 * c1])
+            codes[i] = (words, scales)
+
+        slot_words, slot_scales = {}, {}
+
+        def gather_scales(e):
+            cols = offsets[:, e * LISTC : (e + 1) * LISTC]
+            gs = keep.tile([P, C], U8, name=f"gs{e}", align_bytes=64)
+            nc.vector.tensor_copy(gs[:], x_scales[:].indirect(cols))
+            slot_scales[e] = gs
+
+        def gather_words(e, s):
+            cols = offsets[:, e * LISTC : (e + 1) * LISTC]
+            g = keep.tile([P, C], U32, name=f"g{e}_{s}", align_bytes=64)
+            nc.vector.tensor_copy(g[:], codes[s][0][:].indirect(cols))
+            slot_words[e, s] = g
+
+        accs = {}
+
+        def multiply(i):
+            kind, e, s = steps[i]
+            if kind not in ("w1", "w3"):
+                return
+            if s == 0:
+                accs[kind, e] = [psum.tile([P, 512], F32, name=f"{kind}_{t}", tag=f"{kind}_{t}") for t in range(4)]
+            words, scales = codes[i]
+            for t in range(4):
+                cols = slice(t * P, (t + 1) * P)
+                nc.tensor.matmul_mx(
+                    accs[kind, e][t][:, 0:C],
+                    lhsT=words[:, cols].bitcast(FP8X4),
+                    lhsT_scale=scales[:, cols],
+                    rhs=slot_words[e, s][:].bitcast(FP8X4),
+                    rhs_scale=slot_scales[e][4 * s : P, :],
+                    start=(s == 0),
+                    stop=(s == PASSES - 1),
+                )
+
+        gas, hs = {}, {}
+
+        def gelu(e):
+            ga = act_pool.tile([P, PACK, C], F32, name="ga", tag="ga")
+            for t in range(4):
+                nc.scalar.activation(ga[:, t, :], accs["w1", e][t][:, 0:C], GELU)
+            gas[e] = ga
+
+        def hidden(e):
+            h = act_pool.tile([P, PACK, C], F32, name="h", tag="h")
+            for t in range(4):
+                nc.vector.tensor_tensor(h[:, t, :], accs["w3", e][t][:, 0:C], gas[e][:, t, :], MULT)
+            h_il = act_pool.tile([P, PACK * C], BF16, name="h_il", tag="h_il", align_bytes=64)
+            natural(nc.vector.tensor_copy, h_il, h, 0, C)
+            h_words = act_pool.tile([P, C], U32, name="h_words", tag="h_words", align_bytes=64)
+            h_scales = act_pool.tile([P, C], U8, name="h_scales", tag="h_scales", align_bytes=64)
+            nc.vector.quantize_mx(h_words[:].bitcast(FP8X4), h_scales[:], h_il[:])
+            hs[e] = (h_words, h_scales)
+
+        windows = [keep.tile([P, T], F32, name=f"window{n}") for n in range(4)]
+
+        ys_tiles = {}
+
+        def down(e, n):
+            words, scales = codes[12 + 9 * e]
+            h_words, h_scales = hs[e]
+            cols = slice(n * P, (n + 1) * P)
+            ytag = f"w3_{n}" if e == 0 else f"w1_{n}"
+            y = psum.tile([P, 512], F32, name=ytag, tag=ytag)
+            nc.tensor.matmul_mx(
+                y[:, 0:C],
+                lhsT=words[:, cols].bitcast(FP8X4),
+                lhsT_scale=scales[:, cols],
+                rhs=h_words[:].bitcast(FP8X4),
+                rhs_scale=h_scales[:],
+                start=True,
+                stop=True,
+            )
+            ys = y_pool.tile([P, C], F32, name="ys", tag="ys")
+            nc.scalar.copy(ys[:], y[:, 0:C])
+            ys_tiles[e, n] = ys
+
+        def scatter(e, n):
+            cols = slice(n * P, (n + 1) * P)
+            ys = ys_tiles[e, n]
+            nc.vector.tensor_tensor(
+                windows[n][:].indirect(offsets[:, e * LISTC : (e + 1) * LISTC]), ys[:], gates[e][:, n, :], MULT
+            )
+            if e == E - 1:
+                nc.sync.dma_start(out[cols, :], windows[n][:])
+
+        for i in range(n_steps + 1):
+            if i < n_steps:
+                load(i)
+                round_(i)
+            k = i - 1
+            if k < 0:
+                continue
+            if k == n_steps - 1:
+                hidden(1)
+            quantize(k)
+            if k == 3:
+                gather_scales(0)
+                for s in range(PASSES):
+                    gather_words(0, s)
+            multiply(k)
+            if k == 7:
+                gather_scales(1)
+            if 7 <= k < 11:
+                gather_words(1, k - 7)
+            if k == 10:
+                gelu(0)
+            if k == 12:
+                hidden(0)
+                for n in range(4):
+                    down(0, n)
+            if k == 13:
+                scatter(0, 0)
+            if 13 <= k < 16:
+                scatter(0, k - 12)
+            if k == 19:
+                gelu(1)
+        for n in range(4):
+            down(1, n)
+        for n in range(4):
+            scatter(1, n)

@@ -19,7 +19,8 @@ PACK = 4
 KP = P * PACK
 PASSES = K // KP
 LISTC = C // 16
-VECTOR_SHARE = {("w1", 0): (0, 16, 0, 16), ("w3", 0): (0, 16, 0, 16), ("w1", 1): (0, 16, 0, 16), ("w3", 1): (0, 16, 8, 16)}
+SHARE = [0,0,16,0,20,16,12,32,16,8,20,24,0,0,12,0,0,12,16,8,16,0]
+GA_IN = [10,20]
 
 
 def tile_routed_moe_kernel(tc, xT, w1, w3, w2, gate, offs, out):
@@ -90,19 +91,26 @@ def tile_routed_moe_kernel(tc, xT, w1, w3, w2, gate, offs, out):
             il = il_pool.tile([P, PACK * 512], BF16, name="il", tag="il", align_bytes=64)
             ils[i] = il
             if kind == "x":
-                natural(nc.vector.tensor_copy, il, raw, 0, 192)
-                natural(nc.scalar.copy, il, raw, 192, 512)
+                split = 16 * SHARE[i]
+                if split > 0:
+                    natural(nc.vector.tensor_copy, il, raw, 0, split)
+                if split < 512:
+                    natural(nc.scalar.copy, il, raw, split, 512)
             elif kind == "w2":
-                if e == 0:
-                    natural(nc.vector.tensor_copy, il, raw, 0, 512)
-                else:
-                    natural(nc.scalar.copy, il, raw, 0, 256)
-                    natural(nc.scalar.copy, il, raw, 256, 512)
+                split = 16 * SHARE[i]
+                if split > 0:
+                    natural(nc.vector.tensor_copy, il, raw, 0, split)
+                if e == 1 and split < 256:
+                    natural(nc.scalar.copy, il, raw, split, 256)
+                    split = 256
+                if split < 512:
+                    natural(nc.scalar.copy, il, raw, split, 512)
             else:
-                split = VECTOR_SHARE[kind, e][s]
-                if split:
+                split = SHARE[i]
+                if split > 0:
                     permuted(nc.vector.tensor_copy, il, raw, 0, split)
-                permuted(nc.scalar.copy, il, raw, split, 32)
+                if split < 32:
+                    permuted(nc.scalar.copy, il, raw, split, 32)
 
         def quantize(i):
             kind, e, s = steps[i]
@@ -156,7 +164,7 @@ def tile_routed_moe_kernel(tc, xT, w1, w3, w2, gate, offs, out):
         gas, hs = {}, {}
 
         def gelu(e):
-            ga = act_pool.tile([P, PACK, C], F32, name="ga", tag="ga")
+            ga = raws[GA_IN[e]][:, 0:2, :].rearrange("p a (b c) -> p (a b) c", b=2)
             for t in range(4):
                 nc.scalar.activation(ga[:, t, :], accs["w1", e][t][:, 0:C], GELU)
             gas[e] = ga
@@ -192,15 +200,13 @@ def tile_routed_moe_kernel(tc, xT, w1, w3, w2, gate, offs, out):
                 stop=True,
             )
             ys = y_pool.tile([P, C], F32, name="ys", tag="ys")
-            nc.scalar.copy(ys[:], y[:, 0:C])
+            nc.vector.tensor_tensor(ys[:], y[:, 0:C], gates[e][:, n, :], MULT)
             ys_tiles[e, n] = ys
 
         def scatter(e, n):
             cols = slice(n * P, (n + 1) * P)
             ys = ys_tiles[e, n]
-            nc.vector.tensor_tensor(
-                windows[n][:].indirect(offsets[:, e * LISTC : (e + 1) * LISTC]), ys[:], gates[e][:, n, :], MULT
-            )
+            nc.vector.tensor_copy(windows[n][:].indirect(offsets[:, e * LISTC : (e + 1) * LISTC]), ys[:])
             if e == E - 1:
                 nc.sync.dma_start(out[cols, :], windows[n][:])
 
@@ -221,21 +227,18 @@ def tile_routed_moe_kernel(tc, xT, w1, w3, w2, gate, offs, out):
             multiply(k)
             if k == 7:
                 gather_scales(1)
-            if 7 <= k < 11:
-                gather_words(1, k - 7)
-            if k == 10:
+                for s in range(PASSES):
+                    gather_words(1, s)
+            if k == GA_IN[0]:
                 gelu(0)
             if k == 12:
                 hidden(0)
+            if k == 12:
                 for n in range(4):
                     down(0, n)
-            if k == 13:
-                scatter(0, 0)
-            if 13 <= k < 16:
-                scatter(0, k - 12)
-            if k == 19:
+                    scatter(0, n)
+            if k == GA_IN[1]:
                 gelu(1)
         for n in range(4):
             down(1, n)
-        for n in range(4):
             scatter(1, n)

@@ -19,16 +19,18 @@ PACK = 4
 KP = P * PACK
 PASSES = K // KP
 LISTC = C // 16
-SHARE = [0,0,16,0,20,16,12,32,16,8,20,24,0,0,12,0,0,12,16,8,16,0]
+SHARE = [16,16,16,16,12,12,12,12,12,12,12,12,8,16,0,16,0,8,8,8,16,0]
 GA_IN = [10,20]
+YS_IN = [13,13]
+N128 = [[1,1],[1,1]]
 
 
 def tile_routed_moe_kernel(tc, xT, w1, w3, w2, gate, offs, out):
     nc = tc.nc
     with ExitStack() as ctx:
         keep = ctx.enter_context(tc.tile_pool(name="keep", bufs=1))
-        raw_pool = ctx.enter_context(tc.tile_pool(name="raw", bufs=8))
-        il_pool = ctx.enter_context(tc.tile_pool(name="il", bufs=4))
+        raw_pool = ctx.enter_context(tc.tile_pool(name="raw", bufs=10))
+        il_pool = ctx.enter_context(tc.tile_pool(name="il", bufs=8))
         act_pool = ctx.enter_context(tc.tile_pool(name="act", bufs=2))
         y_pool = ctx.enter_context(tc.tile_pool(name="y", bufs=4))
         psum = ctx.enter_context(tc.psum_pool(name="psum", bufs=1))
@@ -142,56 +144,80 @@ def tile_routed_moe_kernel(tc, xT, w1, w3, w2, gate, offs, out):
 
         accs = {}
 
+        def mx(bank, words, scales, cols, e, s, slots, start, stop):
+            nc.tensor.matmul_mx(
+                bank,
+                lhsT=words[:, cols].bitcast(FP8X4),
+                lhsT_scale=scales[:, cols],
+                rhs=slot_words[e, s][:, slots].bitcast(FP8X4),
+                rhs_scale=slot_scales[e][4 * s : P, slots],
+                start=start,
+                stop=stop,
+            )
+
         def multiply(i):
             kind, e, s = steps[i]
             if kind not in ("w1", "w3"):
+                return
+            if N128[e][0 if kind == "w1" else 1]:
+                if s < PASSES - 1:
+                    return
+                banks = [psum.tile([P, 512], F32, name=f"{kind}_{c}", tag=f"{kind}_{c}") for c in range(2)]
+                accs[kind, e] = banks
+                for c in range(2):
+                    for t in range(4):
+                        for p in range(PASSES):
+                            words, scales = codes[i - PASSES + 1 + p]
+                            mx(banks[c][:, t * P : (t + 1) * P], words, scales, slice(t * P, (t + 1) * P), e, p, slice(c * P, (c + 1) * P), p == 0, p == PASSES - 1)
                 return
             if s == 0:
                 accs[kind, e] = [psum.tile([P, 512], F32, name=f"{kind}_{t}", tag=f"{kind}_{t}") for t in range(4)]
             words, scales = codes[i]
             for t in range(4):
-                cols = slice(t * P, (t + 1) * P)
-                nc.tensor.matmul_mx(
-                    accs[kind, e][t][:, 0:C],
-                    lhsT=words[:, cols].bitcast(FP8X4),
-                    lhsT_scale=scales[:, cols],
-                    rhs=slot_words[e, s][:].bitcast(FP8X4),
-                    rhs_scale=slot_scales[e][4 * s : P, :],
-                    start=(s == 0),
-                    stop=(s == PASSES - 1),
-                )
+                mx(accs[kind, e][t][:, 0:C], words, scales, slice(t * P, (t + 1) * P), e, s, slice(0, C), s == 0, s == PASSES - 1)
 
         gas, hs = {}, {}
 
         def gelu(e):
-            ga = raws[GA_IN[e]][:, 0:2, :].rearrange("p a (b c) -> p (a b) c", b=2)
-            for t in range(4):
-                nc.scalar.activation(ga[:, t, :], accs["w1", e][t][:, 0:C], GELU)
-            gas[e] = ga
+            host = raws[GA_IN[e]]
+            if N128[e][1]:
+                gas[e] = [host[:, 2 * c : 2 * c + 2, 256:512].rearrange("p r (n j) -> p r n j", j=4) for c in range(2)]
+                for c in range(2):
+                    nc.scalar.activation(gas[e][c], accs["w1", e][c][:].rearrange("p (j r n) -> p r n j", j=4, r=2), GELU)
+            else:
+                gas[e] = host[:, :, 256:512]
+                for t in range(4):
+                    nc.scalar.activation(gas[e][:, t, :], accs["w1", e][t][:, 0:C], GELU)
 
         def hidden(e):
-            h = act_pool.tile([P, PACK, C], F32, name="h", tag="h")
-            for t in range(4):
-                nc.vector.tensor_tensor(h[:, t, :], accs["w3", e][t][:, 0:C], gas[e][:, t, :], MULT)
             h_il = act_pool.tile([P, PACK * C], BF16, name="h_il", tag="h_il", align_bytes=64)
-            natural(nc.vector.tensor_copy, h_il, h, 0, C)
             h_words = act_pool.tile([P, C], U32, name="h_words", tag="h_words", align_bytes=64)
             h_scales = act_pool.tile([P, C], U8, name="h_scales", tag="h_scales", align_bytes=64)
+            if N128[e][1]:
+                for c in range(2):
+                    nc.vector.tensor_tensor(
+                        h_il[:, 512 * c : 512 * (c + 1)].rearrange("p (r n j) -> p r n j", r=2, j=4),
+                        accs["w3", e][c][:].rearrange("p (j r n) -> p r n j", j=4, r=2),
+                        gas[e][c],
+                        MULT,
+                    )
+            else:
+                h = act_pool.tile([P, PACK, C], F32, name="h", tag="h")
+                for t in range(4):
+                    nc.vector.tensor_tensor(h[:, t, :], accs["w3", e][t][:, 0:C], gas[e][:, t, :], MULT)
+                natural(nc.vector.tensor_copy, h_il, h, 0, C)
             nc.vector.quantize_mx(h_words[:].bitcast(FP8X4), h_scales[:], h_il[:])
             hs[e] = (h_words, h_scales)
 
         windows = [keep.tile([P, T], F32, name=f"window{n}") for n in range(4)]
-
         ys_tiles = {}
 
-        def down(e, n):
+        def down_mm(e, n, bank):
             words, scales = codes[12 + 9 * e]
             h_words, h_scales = hs[e]
             cols = slice(n * P, (n + 1) * P)
-            ytag = f"w3_{n}" if e == 0 else f"w1_{n}"
-            y = psum.tile([P, 512], F32, name=ytag, tag=ytag)
             nc.tensor.matmul_mx(
-                y[:, 0:C],
+                bank,
                 lhsT=words[:, cols].bitcast(FP8X4),
                 lhsT_scale=scales[:, cols],
                 rhs=h_words[:].bitcast(FP8X4),
@@ -199,16 +225,29 @@ def tile_routed_moe_kernel(tc, xT, w1, w3, w2, gate, offs, out):
                 start=True,
                 stop=True,
             )
+
+        def down0(a):
+            y = psum.tile([P, 512], F32, name=f"w3_{2 + a}", tag=f"w3_{2 + a}")
+            for b in range(2):
+                down_mm(0, 2 * a + b, y[:, b * C : (b + 1) * C])
+            ys = raws[YS_IN[a]][:, 2 * a : 2 * a + 2, 256:512]
+            nc.scalar.copy(ys, y[:].rearrange("p (b c) -> p b c", b=2))
+            for b in range(2):
+                ys_tiles[0, 2 * a + b] = ys[:, b, :]
+
+        def down1(n):
+            y = psum.tile([P, 512], F32, name=f"w1_{n}", tag=f"w1_{n}")
+            down_mm(1, n, y[:, 0:C])
             ys = y_pool.tile([P, C], F32, name="ys", tag="ys")
-            nc.vector.tensor_tensor(ys[:], y[:, 0:C], gates[e][:, n, :], MULT)
-            ys_tiles[e, n] = ys
+            nc.scalar.copy(ys[:], y[:, 0:C])
+            ys_tiles[1, n] = ys[:]
 
         def scatter(e, n):
-            cols = slice(n * P, (n + 1) * P)
-            ys = ys_tiles[e, n]
-            nc.vector.tensor_copy(windows[n][:].indirect(offsets[:, e * LISTC : (e + 1) * LISTC]), ys[:])
+            nc.vector.tensor_tensor(
+                windows[n][:].indirect(offsets[:, e * LISTC : (e + 1) * LISTC]), ys_tiles[e, n], gates[e][:, n, :], MULT
+            )
             if e == E - 1:
-                nc.sync.dma_start(out[cols, :], windows[n][:])
+                nc.sync.dma_start(out[n * P : (n + 1) * P, :], windows[n][:])
 
         for i in range(n_steps + 1):
             if i < n_steps:
@@ -233,12 +272,13 @@ def tile_routed_moe_kernel(tc, xT, w1, w3, w2, gate, offs, out):
                 gelu(0)
             if k == 12:
                 hidden(0)
-            if k == 12:
-                for n in range(4):
-                    down(0, n)
-                    scatter(0, n)
+            for a in range(2):
+                if k == YS_IN[a]:
+                    down0(a)
+                    scatter(0, 2 * a)
+                    scatter(0, 2 * a + 1)
             if k == GA_IN[1]:
                 gelu(1)
         for n in range(4):
-            down(1, n)
+            down1(n)
             scatter(1, n)

@@ -19,10 +19,11 @@ PACK = 4
 KP = P * PACK
 PASSES = K // KP
 LISTC = C // 16
-SHARE = [16,16,16,16,12,12,12,12,12,12,12,12,8,16,0,16,0,8,8,8,16,0]
-GA_IN = [10,20]
+SHARE = [12,12,12,12,16,16,16,16,16,16,16,16,0,16,0,8,0,8,12,16,16,0]
+GA_IN = [11,20]
 YS_IN = [13,13]
-N128 = [[1,1],[1,1]]
+N128 = [[0,0],[0,0]]
+W2_AT = [8,8]
 
 
 def tile_routed_moe_kernel(tc, xT, w1, w3, w2, gate, offs, out):
@@ -56,10 +57,11 @@ def tile_routed_moe_kernel(tc, xT, w1, w3, w2, gate, offs, out):
 
         steps = [("x", 0, s) for s in range(PASSES)]
         for e in range(E):
-            steps += [("w1", e, s) for s in range(PASSES)]
-            steps += [("w3", e, s) for s in range(PASSES)]
-            steps += [("w2", e, 0)]
+            part = [("w1", e, s) for s in range(PASSES)] + [("w3", e, s) for s in range(PASSES)]
+            part.insert(W2_AT[e], ("w2", e, 0))
+            steps += part
         n_steps = len(steps)
+        at = {step: i for i, step in enumerate(steps)}
         dram = {"w1": w1, "w3": w3}
 
         raws, ils, codes = {}, {}, {}
@@ -73,19 +75,21 @@ def tile_routed_moe_kernel(tc, xT, w1, w3, w2, gate, offs, out):
                 rows = w2[e].rearrange("(q t s) n -> s q t n", t=4, s=4)
                 for s in range(4):
                     nc.sync.dma_start(raw[s::4], rows[s])
-                gt = keep.tile([P, 4, C], F32, name=f"gate{e}")
-                nc.sync.dma_start(gt[:], gate[:, e * C : (e + 1) * C].rearrange("(n p) c -> p n c", p=P))
-                gates[e] = gt
                 return
             if kind == "x":
                 src = xT[s * KP : (s + 1) * KP, :].rearrange("(p j) t -> p j t", j=PACK)
             else:
                 src = dram[kind][e, s * KP : (s + 1) * KP, :].rearrange("(p j) c -> p j c", j=PACK)
-            if i == n_steps - 2:
+            if steps[i] == ("w3", 1, 3):
                 nc.sync.dma_start(raw[:, :, 256:], src[:, :, 256:])
                 nc.sync.dma_start(raw[:, :, :256], src[:, :, :256])
             else:
                 nc.sync.dma_start(raw[:], src)
+
+        def load_gate(e):
+            gt = keep.tile([P, 4, C], F32, name=f"gate{e}")
+            nc.sync.dma_start(gt[:], gate[:, e * C : (e + 1) * C].rearrange("(n p) c -> p n c", p=P))
+            gates[e] = gt
 
         def round_(i):
             kind, e, s = steps[i]
@@ -167,7 +171,7 @@ def tile_routed_moe_kernel(tc, xT, w1, w3, w2, gate, offs, out):
                 for c in range(2):
                     for t in range(4):
                         for p in range(PASSES):
-                            words, scales = codes[i - PASSES + 1 + p]
+                            words, scales = codes[at[kind, e, p]]
                             mx(banks[c][:, t * P : (t + 1) * P], words, scales, slice(t * P, (t + 1) * P), e, p, slice(c * P, (c + 1) * P), p == 0, p == PASSES - 1)
                 return
             if s == 0:
@@ -213,7 +217,7 @@ def tile_routed_moe_kernel(tc, xT, w1, w3, w2, gate, offs, out):
         ys_tiles = {}
 
         def down_mm(e, n, bank):
-            words, scales = codes[12 + 9 * e]
+            words, scales = codes[at["w2", e, 0]]
             h_words, h_scales = hs[e]
             cols = slice(n * P, (n + 1) * P)
             nc.tensor.matmul_mx(
@@ -252,11 +256,15 @@ def tile_routed_moe_kernel(tc, xT, w1, w3, w2, gate, offs, out):
         for i in range(n_steps + 1):
             if i < n_steps:
                 load(i)
+                if i == 12:
+                    load_gate(0)
+                if i == n_steps - 1:
+                    load_gate(1)
                 round_(i)
             k = i - 1
             if k < 0:
                 continue
-            if k == n_steps - 1:
+            if k == n_steps - 1 and W2_AT[1] == 8:
                 hidden(1)
             quantize(k)
             if k == 3:
@@ -279,6 +287,8 @@ def tile_routed_moe_kernel(tc, xT, w1, w3, w2, gate, offs, out):
                     scatter(0, 2 * a + 1)
             if k == GA_IN[1]:
                 gelu(1)
+        if W2_AT[1] < 8:
+            hidden(1)
         for n in range(4):
             down1(n)
             scatter(1, n)

@@ -16,209 +16,176 @@ GELU = mybir.ActivationFunctionType.Gelu_apprx_tanh
 
 P = 128
 PACK = 4
-KP = P * PACK
-PASSES = K // KP
-LISTC = C // 16
-SHARE = [12,12,12,12,16,16,16,16,16,16,16,16,0,16,0,8,0,8,12,16,16,0]
-GA_IN = [11,20]
-YS_IN = [13,13]
-N128 = [[0,0],[0,0]]
-W2_AT = [8,8]
+K_PASS = P * PACK
+PASSES = K // K_PASS
+WIDTH = 512
+BLOCKS = WIDTH // P
+BANK = 512
+LIST_COLS = C // 16
+HALF = WIDTH // 2
+
+GROUP = 16
+VECTOR_GROUPS = {
+    ("x", 0): (12, 12, 12, 12),
+    ("w1", 0): (16, 16, 16, 16),
+    ("w3", 0): (16, 16, 16, 16),
+    ("w2", 0): (0,),
+    ("w1", 1): (16, 0, 16, 0),
+    ("w3", 1): (0, 16, 16, 20),
+    ("w2", 1): (0,),
+}
 
 
 def tile_routed_moe_kernel(tc, xT, w1, w3, w2, gate, offs, out):
     nc = tc.nc
+    up_weights = {"w1": w1, "w3": w3}
+
+    stream = [("x", 0, s) for s in range(PASSES)]
+    for e in range(E):
+        stream += [("w1", e, s) for s in range(PASSES)]
+        stream += [("w3", e, s) for s in range(PASSES)]
+        stream += [("w2", e, 0)]
+    last = PASSES - 1
+
     with ExitStack() as ctx:
         keep = ctx.enter_context(tc.tile_pool(name="keep", bufs=1))
         raw_pool = ctx.enter_context(tc.tile_pool(name="raw", bufs=10))
-        il_pool = ctx.enter_context(tc.tile_pool(name="il", bufs=8))
-        act_pool = ctx.enter_context(tc.tile_pool(name="act", bufs=2))
-        y_pool = ctx.enter_context(tc.tile_pool(name="y", bufs=4))
+        rounded_pool = ctx.enter_context(tc.tile_pool(name="rounded", bufs=8))
+        hidden_pool = ctx.enter_context(tc.tile_pool(name="hidden", bufs=1))
+        y_pool = ctx.enter_context(tc.tile_pool(name="y", bufs=BLOCKS))
         psum = ctx.enter_context(tc.psum_pool(name="psum", bufs=1))
 
-        offsets = keep.tile([P, E * LISTC], U16, name="offsets")
+        offsets = keep.tile([P, E * LIST_COLS], U16, name="offsets")
         nc.sync.dma_start(offsets[:], offs)
+
         warm = keep.tile([P, 1], F32, name="warm")
         nc.gpsimd.memset(warm[:], 0.0)
         nc.scalar.activation(warm[:], warm[:], GELU)
+
         x_scales = keep.tile([P, T], U8, name="x_scales", align_bytes=64)
         nc.gpsimd.memset(x_scales[:], 0)
 
-        def natural(eng, il, raw, c0, c1):
-            o = il[:].rearrange("p (c i j) -> p c j i", i=4, j=4)[:, c0 // 4 : c1 // 4]
-            i = raw[:].rearrange("p j (c i) -> p c j i", i=4)[:, c0 // 4 : c1 // 4]
-            eng(o, i)
+        windows = [keep.tile([P, T], F32, name=f"window{n}") for n in range(BLOCKS)]
 
-        def permuted(eng, il, raw, q0, q1):
-            o = il[:].rearrange("p (t q s j) -> p t q j s", t=4, s=4, j=4)[:, :, q0:q1]
-            i = raw[:].rearrange("p j (q t s) -> p t q j s", t=4, s=4)[:, :, q0:q1]
-            eng(o, i)
+        raws, rounded, codes = {}, {}, {}
+        gates, slot_words, slot_scales = {}, {}, {}
+        sums, gelus, hidden_codes, y_slots = {}, {}, {}, {}
 
+        def expert_list(e):
+            return offsets[:, e * LIST_COLS : (e + 1) * LIST_COLS]
 
-        steps = [("x", 0, s) for s in range(PASSES)]
-        for e in range(E):
-            part = [("w1", e, s) for s in range(PASSES)] + [("w3", e, s) for s in range(PASSES)]
-            part.insert(W2_AT[e], ("w2", e, 0))
-            steps += part
-        n_steps = len(steps)
-        at = {step: i for i, step in enumerate(steps)}
-        dram = {"w1": w1, "w3": w3}
-
-        raws, ils, codes = {}, {}, {}
-        gates = {}
-
-        def load(i):
-            kind, e, s = steps[i]
-            raw = raw_pool.tile([P, PACK, 512], F32, name="raw", tag="raw")
-            raws[i] = raw
+        def load(entry):
+            kind, e, s = entry
+            raw = raw_pool.tile([P, PACK, WIDTH], F32, name="raw")
+            raws[entry] = raw
             if kind == "w2":
-                rows = w2[e].rearrange("(q t s) n -> s q t n", t=4, s=4)
-                for s in range(4):
-                    nc.sync.dma_start(raw[s::4], rows[s])
+                rows = w2[e].rearrange("(q t r) n -> r q t n", t=4, r=4)
+                for r in range(4):
+                    nc.sync.dma_start(raw[r::4], rows[r])
+                gt = keep.tile([P, BLOCKS, C], F32, name=f"gate{e}")
+                nc.sync.dma_start(gt[:], gate[:, e * C : (e + 1) * C].rearrange("(n p) c -> p n c", p=P))
+                gates[e] = gt
                 return
-            if kind == "x":
-                src = xT[s * KP : (s + 1) * KP, :].rearrange("(p j) t -> p j t", j=PACK)
-            else:
-                src = dram[kind][e, s * KP : (s + 1) * KP, :].rearrange("(p j) c -> p j c", j=PACK)
-            if steps[i] == ("w3", 1, 3):
-                nc.sync.dma_start(raw[:, :, 256:], src[:, :, 256:])
-                nc.sync.dma_start(raw[:, :, :256], src[:, :, :256])
-            else:
-                nc.sync.dma_start(raw[:], src)
+            source = xT if kind == "x" else up_weights[kind][e]
+            nc.sync.dma_start(raw[:], source[s * K_PASS : (s + 1) * K_PASS, :].rearrange("(p j) c -> p j c", j=PACK))
 
-        def load_gate(e):
-            gt = keep.tile([P, 4, C], F32, name=f"gate{e}")
-            nc.sync.dma_start(gt[:], gate[:, e * C : (e + 1) * C].rearrange("(n p) c -> p n c", p=P))
-            gates[e] = gt
-
-        def round_(i):
-            kind, e, s = steps[i]
-            raw = raws[i]
-            il = il_pool.tile([P, PACK * 512], BF16, name="il", tag="il", align_bytes=64)
-            ils[i] = il
-            if kind == "x":
-                split = 16 * SHARE[i]
-                if split > 0:
-                    natural(nc.vector.tensor_copy, il, raw, 0, split)
-                if split < 512:
-                    natural(nc.scalar.copy, il, raw, split, 512)
-            elif kind == "w2":
-                split = 16 * SHARE[i]
-                if split > 0:
-                    natural(nc.vector.tensor_copy, il, raw, 0, split)
-                if e == 1 and split < 256:
-                    natural(nc.scalar.copy, il, raw, split, 256)
-                    split = 256
-                if split < 512:
-                    natural(nc.scalar.copy, il, raw, split, 512)
-            else:
-                split = SHARE[i]
-                if split > 0:
-                    permuted(nc.vector.tensor_copy, il, raw, 0, split)
-                if split < 32:
-                    permuted(nc.scalar.copy, il, raw, split, 32)
-
-        def quantize(i):
-            kind, e, s = steps[i]
-            il = ils[i]
-            words = keep.tile([P, 512], U32, name=f"words_{kind}_{e}_{s}", align_bytes=64)
-            if kind == "x":
-                scales = x_scales
-                nc.vector.quantize_mx(words[:].bitcast(FP8X4), x_scales[4 * s : P, :], il[:])
-            else:
-                scales = keep.tile([P, 512], U8, name=f"scales_{kind}_{e}_{s}", align_bytes=64)
-                cuts = (0, 256, 512) if kind == "w2" and e == 1 else (0, 512)
-                for c0, c1 in zip(cuts[:-1], cuts[1:]):
-                    nc.vector.quantize_mx(words[:, c0:c1].bitcast(FP8X4), scales[:, c0:c1], il[:, 4 * c0 : 4 * c1])
-            codes[i] = (words, scales)
-
-        slot_words, slot_scales = {}, {}
-
-        def gather_scales(e):
-            cols = offsets[:, e * LISTC : (e + 1) * LISTC]
-            gs = keep.tile([P, C], U8, name=f"gs{e}", align_bytes=64)
-            nc.vector.tensor_copy(gs[:], x_scales[:].indirect(cols))
-            slot_scales[e] = gs
-
-        def gather_words(e, s):
-            cols = offsets[:, e * LISTC : (e + 1) * LISTC]
-            g = keep.tile([P, C], U32, name=f"g{e}_{s}", align_bytes=64)
-            nc.vector.tensor_copy(g[:], codes[s][0][:].indirect(cols))
-            slot_words[e, s] = g
-
-        accs = {}
-
-        def mx(bank, words, scales, cols, e, s, slots, start, stop):
-            nc.tensor.matmul_mx(
-                bank,
-                lhsT=words[:, cols].bitcast(FP8X4),
-                lhsT_scale=scales[:, cols],
-                rhs=slot_words[e, s][:, slots].bitcast(FP8X4),
-                rhs_scale=slot_scales[e][4 * s : P, slots],
-                start=start,
-                stop=stop,
+        def interleave(copy, dst, src, c0, c1):
+            copy(
+                dst[:].rearrange("p (c i j) -> p c j i", i=4, j=PACK)[:, c0 // 4 : c1 // 4],
+                src[:].rearrange("p j (c i) -> p c j i", i=4)[:, c0 // 4 : c1 // 4],
             )
 
-        def multiply(i):
-            kind, e, s = steps[i]
-            if kind not in ("w1", "w3"):
-                return
-            if N128[e][0 if kind == "w1" else 1]:
-                if s < PASSES - 1:
-                    return
-                banks = [psum.tile([P, 512], F32, name=f"{kind}_{c}", tag=f"{kind}_{c}") for c in range(2)]
-                accs[kind, e] = banks
-                for c in range(2):
-                    for t in range(4):
-                        for p in range(PASSES):
-                            words, scales = codes[at[kind, e, p]]
-                            mx(banks[c][:, t * P : (t + 1) * P], words, scales, slice(t * P, (t + 1) * P), e, p, slice(c * P, (c + 1) * P), p == 0, p == PASSES - 1)
-                return
-            if s == 0:
-                accs[kind, e] = [psum.tile([P, 512], F32, name=f"{kind}_{t}", tag=f"{kind}_{t}") for t in range(4)]
-            words, scales = codes[i]
-            for t in range(4):
-                mx(accs[kind, e][t][:, 0:C], words, scales, slice(t * P, (t + 1) * P), e, s, slice(0, C), s == 0, s == PASSES - 1)
+        def interleave_permuted(copy, dst, src, q0, q1):
+            copy(
+                dst[:].rearrange("p (t q r j) -> p t q j r", t=4, r=4, j=PACK)[:, :, q0:q1],
+                src[:].rearrange("p j (q t r) -> p t q j r", t=4, r=4)[:, :, q0:q1],
+            )
 
-        gas, hs = {}, {}
+        def round_to_bf16(entry):
+            kind, e, s = entry
+            raw = raws[entry]
+            dst = rounded_pool.tile([P, PACK * WIDTH], BF16, name="dst", align_bytes=64)
+            rounded[entry] = dst
+            on_vector = VECTOR_GROUPS[kind, e][s]
+            if kind in up_weights:
+                if on_vector > 0:
+                    interleave_permuted(nc.vector.tensor_copy, dst, raw, 0, on_vector)
+                interleave_permuted(nc.scalar.copy, dst, raw, on_vector, WIDTH // GROUP)
+            else:
+                cuts = (0, HALF, WIDTH) if entry == stream[-1] else (on_vector * GROUP, WIDTH)
+                if on_vector > 0:
+                    interleave(nc.vector.tensor_copy, dst, raw, 0, on_vector * GROUP)
+                for c0, c1 in zip(cuts[:-1], cuts[1:]):
+                    interleave(nc.scalar.copy, dst, raw, c0, c1)
+
+        def quantize(entry):
+            kind, e, s = entry
+            src = rounded[entry]
+            if kind == "w2":
+                words = hidden_pool.tile([P, WIDTH], U32, name="w2_words", tag="h", align_bytes=64)
+                scales = hidden_pool.tile([P, WIDTH], U8, name="w2_scales", tag="h_rounded", align_bytes=64)
+            else:
+                words = keep.tile([P, WIDTH], U32, name=f"{kind}_words{e}_{s}", align_bytes=64)
+            if kind == "x":
+                scales = x_scales
+                nc.vector.quantize_mx(words[:].bitcast(FP8X4), x_scales[4 * s : P, :], src[:])
+            else:
+                if kind != "w2":
+                    scales = keep.tile([P, WIDTH], U8, name=f"{kind}_scales{e}_{s}", align_bytes=64)
+                cuts = (0, HALF, WIDTH) if entry in stream[-2:] else (0, WIDTH)
+                for c0, c1 in zip(cuts[:-1], cuts[1:]):
+                    nc.vector.quantize_mx(
+                        words[:, c0:c1].bitcast(FP8X4), scales[:, c0:c1], src[:, PACK * c0 : PACK * c1]
+                    )
+            codes[entry] = (words, scales)
+
+        def gather(e):
+            bytes_of_slots = keep.tile([P, C], U8, name=f"slot_scales{e}", align_bytes=64)
+            nc.vector.tensor_copy(bytes_of_slots[:], x_scales[:].indirect(expert_list(e)))
+            slot_scales[e] = bytes_of_slots
+            for s in range(PASSES):
+                words_of_slots = keep.tile([P, C], U32, name=f"slot_words{e}_{s}", align_bytes=64)
+                nc.vector.tensor_copy(words_of_slots[:], codes["x", 0, s][0][:].indirect(expert_list(e)))
+                slot_words[e, s] = words_of_slots
+
+        def multiply_up(entry):
+            kind, e, s = entry
+            if s == 0:
+                sums[kind, e] = [
+                    psum.tile([P, BANK], F32, name=f"{kind}_bank{t}", tag=f"{kind}_bank{t}") for t in range(BLOCKS)
+                ]
+            words, scales = codes[entry]
+            for t in range(BLOCKS):
+                cols = slice(t * P, (t + 1) * P)
+                nc.tensor.matmul_mx(
+                    sums[kind, e][t][:, 0:C],
+                    lhsT=words[:, cols].bitcast(FP8X4),
+                    lhsT_scale=scales[:, cols],
+                    rhs=slot_words[e, s][:].bitcast(FP8X4),
+                    rhs_scale=slot_scales[e][4 * s : P, :],
+                    start=(s == 0),
+                    stop=(s == last),
+                )
 
         def gelu(e):
-            host = raws[GA_IN[e]]
-            if N128[e][1]:
-                gas[e] = [host[:, 2 * c : 2 * c + 2, 256:512].rearrange("p r (n j) -> p r n j", j=4) for c in range(2)]
-                for c in range(2):
-                    nc.scalar.activation(gas[e][c], accs["w1", e][c][:].rearrange("p (j r n) -> p r n j", j=4, r=2), GELU)
-            else:
-                gas[e] = host[:, :, 256:512]
-                for t in range(4):
-                    nc.scalar.activation(gas[e][:, t, :], accs["w1", e][t][:, 0:C], GELU)
+            gelus[e] = raws["w3", e, last][:, :, HALF:WIDTH]
+            for t in range(BLOCKS):
+                nc.scalar.activation(gelus[e][:, t, :], sums["w1", e][t][:, 0:C], GELU)
 
         def hidden(e):
-            h_il = act_pool.tile([P, PACK * C], BF16, name="h_il", tag="h_il", align_bytes=64)
-            h_words = act_pool.tile([P, C], U32, name="h_words", tag="h_words", align_bytes=64)
-            h_scales = act_pool.tile([P, C], U8, name="h_scales", tag="h_scales", align_bytes=64)
-            if N128[e][1]:
-                for c in range(2):
-                    nc.vector.tensor_tensor(
-                        h_il[:, 512 * c : 512 * (c + 1)].rearrange("p (r n j) -> p r n j", r=2, j=4),
-                        accs["w3", e][c][:].rearrange("p (j r n) -> p r n j", j=4, r=2),
-                        gas[e][c],
-                        MULT,
-                    )
-            else:
-                h = act_pool.tile([P, PACK, C], F32, name="h", tag="h")
-                for t in range(4):
-                    nc.vector.tensor_tensor(h[:, t, :], accs["w3", e][t][:, 0:C], gas[e][:, t, :], MULT)
-                natural(nc.vector.tensor_copy, h_il, h, 0, C)
-            nc.vector.quantize_mx(h_words[:].bitcast(FP8X4), h_scales[:], h_il[:])
-            hs[e] = (h_words, h_scales)
+            h = hidden_pool.tile([P, PACK, C], F32, name="h", tag="h", align_bytes=64)
+            for t in range(BLOCKS):
+                nc.vector.tensor_tensor(h[:, t, :], sums["w3", e][t][:, 0:C], gelus[e][:, t, :], MULT)
+            h_rounded = hidden_pool.tile([P, PACK * C], BF16, name="h_rounded", tag="h_rounded", align_bytes=64)
+            interleave(nc.vector.tensor_copy, h_rounded, h, 0, C)
+            h_words = hidden_pool.tile([P, C], U32, name="h_words", align_bytes=64)
+            h_scales = hidden_pool.tile([P, C], U8, name="h_scales", align_bytes=64)
+            nc.vector.quantize_mx(h_words[:].bitcast(FP8X4), h_scales[:], h_rounded[:])
+            hidden_codes[e] = (h_words, h_scales)
 
-        windows = [keep.tile([P, T], F32, name=f"window{n}") for n in range(4)]
-        ys_tiles = {}
-
-        def down_mm(e, n, bank):
-            words, scales = codes[at["w2", e, 0]]
-            h_words, h_scales = hs[e]
+        def multiply_down(e, n, bank):
+            words, scales = codes["w2", e, 0]
+            h_words, h_scales = hidden_codes[e]
             cols = slice(n * P, (n + 1) * P)
             nc.tensor.matmul_mx(
                 bank,
@@ -230,65 +197,52 @@ def tile_routed_moe_kernel(tc, xT, w1, w3, w2, gate, offs, out):
                 stop=True,
             )
 
-        def down0(a):
-            y = psum.tile([P, 512], F32, name=f"w3_{2 + a}", tag=f"w3_{2 + a}")
+        def down_in_pairs(e, n):
+            tag = f"w3_bank{2 + n // 2}"
+            y = psum.tile([P, BANK], F32, name=tag, tag=tag)
             for b in range(2):
-                down_mm(0, 2 * a + b, y[:, b * C : (b + 1) * C])
-            ys = raws[YS_IN[a]][:, 2 * a : 2 * a + 2, 256:512]
-            nc.scalar.copy(ys, y[:].rearrange("p (b c) -> p b c", b=2))
+                multiply_down(e, n + b, y[:, b * C : (b + 1) * C])
+            y_sbuf = raws["w1", e + 1, 0][:, n : n + 2, HALF:WIDTH]
+            nc.scalar.copy(y_sbuf, y[:].rearrange("p (b c) -> p b c", b=2))
             for b in range(2):
-                ys_tiles[0, 2 * a + b] = ys[:, b, :]
+                y_slots[e, n + b] = y_sbuf[:, b, :]
 
-        def down1(n):
-            y = psum.tile([P, 512], F32, name=f"w1_{n}", tag=f"w1_{n}")
-            down_mm(1, n, y[:, 0:C])
-            ys = y_pool.tile([P, C], F32, name="ys", tag="ys")
-            nc.scalar.copy(ys[:], y[:, 0:C])
-            ys_tiles[1, n] = ys[:]
+        def down(e, n):
+            tag = f"w1_bank{n}"
+            y = psum.tile([P, BANK], F32, name=tag, tag=tag)
+            multiply_down(e, n, y[:, 0:C])
+            y_sbuf = y_pool.tile([P, C], F32, name="y_sbuf")
+            nc.scalar.copy(y_sbuf[:], y[:, 0:C])
+            y_slots[e, n] = y_sbuf[:]
 
         def scatter(e, n):
-            nc.vector.tensor_tensor(
-                windows[n][:].indirect(offsets[:, e * LISTC : (e + 1) * LISTC]), ys_tiles[e, n], gates[e][:, n, :], MULT
-            )
-            if e == E - 1:
-                nc.sync.dma_start(out[n * P : (n + 1) * P, :], windows[n][:])
+            nc.vector.tensor_tensor(windows[n][:].indirect(expert_list(e)), y_slots[e, n], gates[e][:, n, :], MULT)
 
-        for i in range(n_steps + 1):
-            if i < n_steps:
-                load(i)
-                if i == 12:
-                    load_gate(0)
-                if i == n_steps - 1:
-                    load_gate(1)
-                round_(i)
-            k = i - 1
-            if k < 0:
-                continue
-            if k == n_steps - 1 and W2_AT[1] == 8:
-                hidden(1)
-            quantize(k)
-            if k == 3:
-                gather_scales(0)
-                for s in range(PASSES):
-                    gather_words(0, s)
-            multiply(k)
-            if k == 7:
-                gather_scales(1)
-                for s in range(PASSES):
-                    gather_words(1, s)
-            if k == GA_IN[0]:
-                gelu(0)
-            if k == 12:
-                hidden(0)
-            for a in range(2):
-                if k == YS_IN[a]:
-                    down0(a)
-                    scatter(0, 2 * a)
-                    scatter(0, 2 * a + 1)
-            if k == GA_IN[1]:
-                gelu(1)
-        if W2_AT[1] < 8:
-            hidden(1)
-        for n in range(4):
-            down1(n)
+        load(stream[0])
+        round_to_bf16(stream[0])
+        for i, entry in enumerate(stream):
+            if i + 1 < len(stream):
+                load(stream[i + 1])
+                round_to_bf16(stream[i + 1])
+            kind, e, s = entry
+            if kind == "w2":
+                hidden(e)
+            quantize(entry)
+            if entry == ("x", 0, last):
+                gather(0)
+            if kind in up_weights:
+                multiply_up(entry)
+            if entry == ("w1", 0, last):
+                gather(1)
+            if kind == "w3" and s == last:
+                gelu(e)
+            if entry == ("w1", 1, 0):
+                for n in range(0, BLOCKS, 2):
+                    down_in_pairs(0, n)
+                    scatter(0, n)
+                    scatter(0, n + 1)
+
+        for n in range(BLOCKS):
+            down(1, n)
             scatter(1, n)
+            nc.sync.dma_start(out[n * P : (n + 1) * P, :], windows[n][:])

from contextlib import ExitStack

import concourse.mybir as mybir

K, T, E, C, H, N = 2048, 512, 2, 256, 512, 512
FLOPS = 2 * E * C * (2 * K * H + H * N)

F32 = mybir.dt.float32
BF16 = mybir.dt.bfloat16
U32 = mybir.dt.uint32
U16 = mybir.dt.uint16
U8 = mybir.dt.uint8
FP8X4 = mybir.dt.float8_e4m3fn_x4
MULT = mybir.AluOpType.mult
GELU = mybir.ActivationFunctionType.Gelu_apprx_tanh

P = 128
PACK = 4
K_PASS = P * PACK
PASSES = K // K_PASS
WIDTH = 512
BLOCKS = WIDTH // P
BANK = 512
LIST_COLS = C // 16
HALF = WIDTH // 2

GROUP = 16
VECTOR_GROUPS = {
    ("x", 0): (12, 12, 12, 12),
    ("w1", 0): (16, 16, 16, 16),
    ("w3", 0): (16, 16, 16, 16),
    ("w2", 0): (0,),
    ("w1", 1): (16, 0, 16, 0),
    ("w3", 1): (0, 16, 16, 20),
    ("w2", 1): (0,),
}


def tile_routed_moe_kernel(tc, xT, w1, w3, w2, gate, offs, out):
    nc = tc.nc
    up_weights = {"w1": w1, "w3": w3}

    stream = [("x", 0, s) for s in range(PASSES)]
    for e in range(E):
        stream += [("w1", e, s) for s in range(PASSES)]
        stream += [("w3", e, s) for s in range(PASSES)]
        stream += [("w2", e, 0)]
    last = PASSES - 1

    with ExitStack() as ctx:
        keep = ctx.enter_context(tc.tile_pool(name="keep", bufs=1))
        raw_pool = ctx.enter_context(tc.tile_pool(name="raw", bufs=10))
        rounded_pool = ctx.enter_context(tc.tile_pool(name="rounded", bufs=8))
        hidden_pool = ctx.enter_context(tc.tile_pool(name="hidden", bufs=1))
        y_pool = ctx.enter_context(tc.tile_pool(name="y", bufs=BLOCKS))
        psum = ctx.enter_context(tc.psum_pool(name="psum", bufs=1))

        offsets = keep.tile([P, E * LIST_COLS], U16, name="offsets")
        nc.sync.dma_start(offsets[:], offs)

        warm = keep.tile([P, 1], F32, name="warm")
        nc.gpsimd.memset(warm[:], 0.0)
        nc.scalar.activation(warm[:], warm[:], GELU)

        x_scales = keep.tile([P, T], U8, name="x_scales", align_bytes=64)
        nc.gpsimd.memset(x_scales[:], 0)

        windows = [keep.tile([P, T], F32, name=f"window{n}") for n in range(BLOCKS)]

        raws, rounded, codes = {}, {}, {}
        gates, slot_words, slot_scales = {}, {}, {}
        sums, gelus, hidden_codes, y_slots = {}, {}, {}, {}

        def expert_list(e):
            return offsets[:, e * LIST_COLS : (e + 1) * LIST_COLS]

        def load(entry):
            kind, e, s = entry
            raw = raw_pool.tile([P, PACK, WIDTH], F32, name="raw")
            raws[entry] = raw
            if kind == "w2":
                rows = w2[e].rearrange("(q t r) n -> r q t n", t=4, r=4)
                for r in range(4):
                    nc.sync.dma_start(raw[r::4], rows[r])
                gt = keep.tile([P, BLOCKS, C], F32, name=f"gate{e}")
                nc.sync.dma_start(gt[:], gate[:, e * C : (e + 1) * C].rearrange("(n p) c -> p n c", p=P))
                gates[e] = gt
                return
            source = xT if kind == "x" else up_weights[kind][e]
            nc.sync.dma_start(raw[:], source[s * K_PASS : (s + 1) * K_PASS, :].rearrange("(p j) c -> p j c", j=PACK))

        def interleave(copy, dst, src, c0, c1):
            copy(
                dst[:].rearrange("p (c i j) -> p c j i", i=4, j=PACK)[:, c0 // 4 : c1 // 4],
                src[:].rearrange("p j (c i) -> p c j i", i=4)[:, c0 // 4 : c1 // 4],
            )

        def interleave_permuted(copy, dst, src, q0, q1):
            copy(
                dst[:].rearrange("p (t q r j) -> p t q j r", t=4, r=4, j=PACK)[:, :, q0:q1],
                src[:].rearrange("p j (q t r) -> p t q j r", t=4, r=4)[:, :, q0:q1],
            )

        def round_to_bf16(entry):
            kind, e, s = entry
            raw = raws[entry]
            dst = rounded_pool.tile([P, PACK * WIDTH], BF16, name="dst", align_bytes=64)
            rounded[entry] = dst
            on_vector = VECTOR_GROUPS[kind, e][s]
            if kind in up_weights:
                if on_vector > 0:
                    interleave_permuted(nc.vector.tensor_copy, dst, raw, 0, on_vector)
                interleave_permuted(nc.scalar.copy, dst, raw, on_vector, WIDTH // GROUP)
            else:
                cuts = (0, HALF, WIDTH) if entry == stream[-1] else (on_vector * GROUP, WIDTH)
                if on_vector > 0:
                    interleave(nc.vector.tensor_copy, dst, raw, 0, on_vector * GROUP)
                for c0, c1 in zip(cuts[:-1], cuts[1:]):
                    interleave(nc.scalar.copy, dst, raw, c0, c1)

        def quantize(entry):
            kind, e, s = entry
            src = rounded[entry]
            if kind == "w2":
                words = hidden_pool.tile([P, WIDTH], U32, name="w2_words", tag="h", align_bytes=64)
                scales = hidden_pool.tile([P, WIDTH], U8, name="w2_scales", tag="h_rounded", align_bytes=64)
            else:
                words = keep.tile([P, WIDTH], U32, name=f"{kind}_words{e}_{s}", align_bytes=64)
            if kind == "x":
                scales = x_scales
                nc.vector.quantize_mx(words[:].bitcast(FP8X4), x_scales[4 * s : P, :], src[:])
            else:
                if kind != "w2":
                    scales = keep.tile([P, WIDTH], U8, name=f"{kind}_scales{e}_{s}", align_bytes=64)
                cuts = (0, HALF, WIDTH) if entry in stream[-2:] else (0, WIDTH)
                for c0, c1 in zip(cuts[:-1], cuts[1:]):
                    nc.vector.quantize_mx(
                        words[:, c0:c1].bitcast(FP8X4), scales[:, c0:c1], src[:, PACK * c0 : PACK * c1]
                    )
            codes[entry] = (words, scales)

        def gather(e):
            bytes_of_slots = keep.tile([P, C], U8, name=f"slot_scales{e}", align_bytes=64)
            nc.vector.tensor_copy(bytes_of_slots[:], x_scales[:].indirect(expert_list(e)))
            slot_scales[e] = bytes_of_slots
            for s in range(PASSES):
                words_of_slots = keep.tile([P, C], U32, name=f"slot_words{e}_{s}", align_bytes=64)
                nc.vector.tensor_copy(words_of_slots[:], codes["x", 0, s][0][:].indirect(expert_list(e)))
                slot_words[e, s] = words_of_slots

        def multiply_up(entry):
            kind, e, s = entry
            if s == 0:
                sums[kind, e] = [
                    psum.tile([P, BANK], F32, name=f"{kind}_bank{t}", tag=f"{kind}_bank{t}") for t in range(BLOCKS)
                ]
            words, scales = codes[entry]
            for t in range(BLOCKS):
                cols = slice(t * P, (t + 1) * P)
                nc.tensor.matmul_mx(
                    sums[kind, e][t][:, 0:C],
                    lhsT=words[:, cols].bitcast(FP8X4),
                    lhsT_scale=scales[:, cols],
                    rhs=slot_words[e, s][:].bitcast(FP8X4),
                    rhs_scale=slot_scales[e][4 * s : P, :],
                    start=(s == 0),
                    stop=(s == last),
                )

        def gelu(e):
            gelus[e] = raws["w3", e, last][:, :, HALF:WIDTH]
            for t in range(BLOCKS):
                nc.scalar.activation(gelus[e][:, t, :], sums["w1", e][t][:, 0:C], GELU)

        def hidden(e):
            h = hidden_pool.tile([P, PACK, C], F32, name="h", tag="h", align_bytes=64)
            for t in range(BLOCKS):
                nc.vector.tensor_tensor(h[:, t, :], sums["w3", e][t][:, 0:C], gelus[e][:, t, :], MULT)
            h_rounded = hidden_pool.tile([P, PACK * C], BF16, name="h_rounded", tag="h_rounded", align_bytes=64)
            interleave(nc.vector.tensor_copy, h_rounded, h, 0, C)
            h_words = hidden_pool.tile([P, C], U32, name="h_words", align_bytes=64)
            h_scales = hidden_pool.tile([P, C], U8, name="h_scales", align_bytes=64)
            nc.vector.quantize_mx(h_words[:].bitcast(FP8X4), h_scales[:], h_rounded[:])
            hidden_codes[e] = (h_words, h_scales)

        def multiply_down(e, n, bank):
            words, scales = codes["w2", e, 0]
            h_words, h_scales = hidden_codes[e]
            cols = slice(n * P, (n + 1) * P)
            nc.tensor.matmul_mx(
                bank,
                lhsT=words[:, cols].bitcast(FP8X4),
                lhsT_scale=scales[:, cols],
                rhs=h_words[:].bitcast(FP8X4),
                rhs_scale=h_scales[:],
                start=True,
                stop=True,
            )

        def down_in_pairs(e, n):
            tag = f"w3_bank{2 + n // 2}"
            y = psum.tile([P, BANK], F32, name=tag, tag=tag)
            for b in range(2):
                multiply_down(e, n + b, y[:, b * C : (b + 1) * C])
            y_sbuf = raws["w1", e + 1, 0][:, n : n + 2, HALF:WIDTH]
            nc.scalar.copy(y_sbuf, y[:].rearrange("p (b c) -> p b c", b=2))
            for b in range(2):
                y_slots[e, n + b] = y_sbuf[:, b, :]

        def down(e, n):
            tag = f"w1_bank{n}"
            y = psum.tile([P, BANK], F32, name=tag, tag=tag)
            multiply_down(e, n, y[:, 0:C])
            y_sbuf = y_pool.tile([P, C], F32, name="y_sbuf")
            nc.scalar.copy(y_sbuf[:], y[:, 0:C])
            y_slots[e, n] = y_sbuf[:]

        def scatter(e, n):
            nc.vector.tensor_tensor(windows[n][:].indirect(expert_list(e)), y_slots[e, n], gates[e][:, n, :], MULT)

        load(stream[0])
        round_to_bf16(stream[0])
        for i, entry in enumerate(stream):
            if i + 1 < len(stream):
                load(stream[i + 1])
                round_to_bf16(stream[i + 1])
            kind, e, s = entry
            if kind == "w2":
                hidden(e)
            quantize(entry)
            if entry == ("x", 0, last):
                gather(0)
            if kind in up_weights:
                multiply_up(entry)
            if entry == ("w1", 0, last):
                gather(1)
            if kind == "w3" and s == last:
                gelu(e)
            if entry == ("w1", 1, 0):
                for n in range(0, BLOCKS, 2):
                    down_in_pairs(0, n)
                    scatter(0, n)
                    scatter(0, n + 1)

        for n in range(BLOCKS):
            down(1, n)
            scatter(1, n)
            nc.sync.dma_start(out[n * P : (n + 1) * P, :], windows[n][:])
